import numpy as np
import ml_dtypes


def mxq(x, axis, fmt="e4m3"):
    dtype, down = {"e4m3": (ml_dtypes.float8_e4m3fn, 7), "e5m2": (ml_dtypes.float8_e5m2, 14)}[fmt]
    v = np.moveaxis(np.asarray(x, np.float32).astype(ml_dtypes.bfloat16).astype(np.float64), axis, -1)
    blocks = v.reshape(v.shape[:-1] + (-1, 32))
    amax = np.abs(blocks).max(-1, keepdims=True)
    byte = np.maximum(np.where(amax > 0, np.frexp(amax)[1] - 1 + 127, 0) - down, 1)
    scale = np.exp2(byte - 127.0)
    codes = (blocks / scale).astype(np.float32).astype(dtype).astype(np.float64)
    return np.moveaxis((codes * scale).reshape(v.shape), -1, axis)


WIDE = False


def mx_kscale(k):
    if not WIDE:
        return np.ones(k)
    levels = np.array([10, -10, 5, -5, 0])
    if k % 512:
        return np.exp2(np.random.permutation(np.resize(levels, k // 32))).repeat(32)
    a = np.empty((k // 512, 16))
    for p in range(k // 512):
        a[p, :8] = np.random.permutation(np.resize(levels, 8))
        for g in range(8):
            far = levels[np.abs(levels - a[p, g]) >= 10]
            a[p, g + 8] = far[np.random.randint(len(far))]
    return np.exp2(a.ravel()).repeat(32)


def f64(x):
    return np.asarray(x).astype(np.float64)


def striped(idx):
    return np.tile(idx.reshape(-1, 16).T, (8, 1)).astype(np.uint16)


def unstriped(offs):
    return offs[:16].T.reshape(-1).astype(np.int64)


def striped8(idx):
    return np.concatenate([x.reshape(-1, 16).T for x in idx]).astype(np.uint16)


def runs(offs, k):
    lists = np.stack([offs[16 * r : 16 * r + 16].T.reshape(-1) for r in range(8)]).astype(np.int64)
    return lists[np.arange(k) % 512 // 64]


def pack_weight(w):
    k, n = w.shape
    w = f64(np.asarray(w, np.float32).astype(ml_dtypes.bfloat16)).reshape(k // 32, 32, n)
    amax = np.abs(w).max(1)
    byte = np.clip(np.where(amax > 0, np.frexp(amax)[1] - 1 + 127 - 7, 1), 1, 254)
    scaled = (w * np.exp2(127.0 - byte)[:, None, :]).reshape(k, n).astype(np.float32)
    words = np.ascontiguousarray(scaled.reshape(k // 512, 128, 4, n).transpose(0, 1, 3, 2)).astype(ml_dtypes.float8_e4m3fn).view(np.uint8)
    return words, np.ascontiguousarray(byte.astype(np.uint8).reshape(k // 512, 16, n))


def unpack_weight(words, scales):
    g, p, n, _ = words.shape
    vals = np.ascontiguousarray(words).view(ml_dtypes.float8_e4m3fn).astype(np.float64) * np.repeat(np.exp2(scales.astype(np.float64) - 127.0), 8, axis=1)[..., None]
    return vals.transpose(0, 1, 3, 2).reshape(g * 512, n)


E2M1 = np.array([0.0, 0.5, 1.0, 1.5, 2.0, 3.0, 4.0, 6.0, -0.0, -0.5, -1.0, -1.5, -2.0, -3.0, -4.0, -6.0])


def pack_fp4(w):
    k, n = w.shape
    w = f64(np.asarray(w, np.float32).astype(ml_dtypes.bfloat16)).reshape(k // 32, 32, n)
    amax = np.abs(w).max(1)
    mant, ex = np.frexp(amax / 6.0)
    byte = np.clip(np.where(amax > 0, np.where(mant > 0.5, ex, ex - 1) + 127, 1), 1, 254)
    scaled = (w * np.exp2(127.0 - byte)[:, None, :]).reshape(k, n).astype(np.float32)
    c = np.ascontiguousarray(scaled.reshape(k // 512, 128, 4, n).transpose(0, 1, 3, 2)).astype(ml_dtypes.float4_e2m1fn).view(np.uint8) & 0xF
    words = (c[..., 0::2] | (c[..., 1::2] << 4)).reshape(k // 512, 128, 2 * n)
    return np.ascontiguousarray(words), np.ascontiguousarray(byte.astype(np.uint8).reshape(k // 512, 16, n))


def unpack_fp4(words, scales):
    g, _, n = scales.shape
    words = np.ascontiguousarray(words).reshape(g, 128, n, 2)
    nib = np.empty((g, 128, n, 4), np.uint8)
    nib[..., 0::2] = words & 0xF
    nib[..., 1::2] = words >> 4
    vals = E2M1[nib] * np.repeat(np.exp2(scales.astype(np.float64) - 127.0), 8, axis=1)[..., None]
    return vals.transpose(0, 1, 3, 2).reshape(g * 512, n)


def planes(y):
    n, m = y.shape
    v = y.astype(np.float32).astype(ml_dtypes.bfloat16).astype(np.float64).reshape(n // 32, 32, m)
    top = np.abs(v).max(1)
    byte = np.clip(np.where(top > 0, np.frexp(top)[1] - 1 + 127 - 7, 1), 1, 254)
    codes = (v * np.exp2(127.0 - byte)[:, None, :]).reshape(n, m).astype(np.float32).astype(ml_dtypes.float8_e4m3fn).view(np.uint8)
    words = codes.reshape(n // 512, 128, 4, m).transpose(0, 1, 3, 2)
    return np.ascontiguousarray(words), np.ascontiguousarray(byte.astype(np.uint8).reshape(n // 512, 16, m))


K, T, S, V, H, J = 512, 2048, 512, 512, 512, 512


def setup_inputs():
    n = np.random.standard_normal
    s = mx_kscale(K)[:, None]
    u = mx_kscale(S)
    packed_xT = pack_weight(n((K, T)) * s)
    packed_w1 = pack_fp4(n((K, H)) / np.sqrt(K) / s)
    packed_w2 = pack_fp4(n((K, H)) / np.sqrt(K) / s)
    return {
        "x_words": packed_xT[0],
        "x_scales": packed_xT[1],
        "w1_words": packed_w1[0],
        "w1_scales": packed_w1[1],
        "w2_words": packed_w2[0],
        "w2_scales": packed_w2[1],
        "ga": (np.random.uniform(0.5, 1.5, (H, 1)) * u[:, None]).astype(np.float32),
        "gb": (np.random.uniform(0.5, 1.5, (H, 1)) / u[:, None]).astype(np.float32),
        "tab": n((S, J)).astype(np.float32),
        "offs": striped(np.random.permutation(T)[:S]),
        "two": striped(np.random.permutation(T)[:V]),
        "n1": striped8(np.stack([np.random.permutation(S) for _ in range(8)])),
        "n2": striped8(np.stack([np.random.permutation(S) for _ in range(8)])),
        "n3": striped8(np.stack([np.random.permutation(V) for _ in range(8)])),
        "n4": striped8(np.stack([np.random.permutation(V) for _ in range(8)])),
        "n5": striped8(np.random.randint(0, J, (8, V))),
        "n6": striped8(np.random.randint(0, J, (8, V))),
        "n7": striped8(np.stack([np.random.permutation(V) for _ in range(8)])),
    }


def reference(x_words, x_scales, w1_words, w1_scales, w2_words, w2_scales, ga, gb, tab, offs, two, n1, n2, n3, n4, n5, n6, n7):
    xq = unpack_weight(x_words, x_scales)[:, unstriped(offs)]
    a = unpack_fp4(w1_words, w1_scales).T @ xq
    st = a + 0.5 * (a[np.arange(H)[:, None], runs(n1, H)])
    z = f64(ga) * (st - (st[np.arange(H)[:, None], runs(n2, H)]))
    x_two = unpack_weight(x_words, x_scales)[:, unstriped(two)]
    b = unpack_fp4(w2_words, w2_scales).T @ x_two
    z2 = f64(gb) * (np.maximum(b[np.arange(H)[:, None], runs(n3, H)], b[np.arange(H)[:, None], runs(n4, H)]) - (0.75 * b))
    s = 0.0625 * ((mxq(z, 0, "e4m3").T @ mxq(z2, 0, "e4m3")))
    out_0 = (s[np.arange(S)[:, None], runs(n7, S)]) * (f64(tab)[np.arange(S)[:, None], runs(n5, S)]) + f64(tab)[np.arange(S)[:, None], runs(n6, S)]
    return (out_0,) + planes(out_0)

@@ -1,0 +1,266 @@
+from contextlib import ExitStack
+
+import concourse.mybir as mybir
+from concourse.masks import make_identity
+
+K, T, S, V, H, J = 512, 2048, 512, 512, 512, 512
+FLOPS = 2 * K * H * S + 2 * K * H * V + 2 * H * S * V
+
+F32 = mybir.dt.float32
+BF16 = mybir.dt.bfloat16
+I32 = mybir.dt.int32
+U32 = mybir.dt.uint32
+U16 = mybir.dt.uint16
+U8 = mybir.dt.uint8
+FP8X4 = mybir.dt.float8_e4m3fn_x4
+FP4X4 = mybir.dt.float4_e2m1fn_x4
+ALU = mybir.AluOpType
+ACT = mybir.ActivationFunctionType
+
+P = 128
+PACK = 4
+QUADS = 4
+COLS = 512
+HALF = COLS // 2
+PER_COL = 16
+
+
+def tile_picked_kqhopoverkinda_none_po_kernel(
+    tc, x_words, x_scales, w1_words, w1_scales, w2_words, w2_scales, ga, gb, tab,
+    offs, two, n1, n2, n3, n4, n5, n6, n7, out_0, out_1, out_2,
+):
+    nc = tc.nc
+    with ExitStack() as ctx:
+        lists = ctx.enter_context(tc.tile_pool(name="lists", bufs=1))
+        keep = ctx.enter_context(tc.tile_pool(name="keep", bufs=1))
+        psum = ctx.enter_context(tc.psum_pool(name="psum", bufs=8))
+
+        def load_list(source, name):
+            tile = lists.tile([P, COLS // PER_COL], U16, name=name)
+            nc.sync.dma_start(tile[:], source)
+            return tile
+
+        def half_of(offsets, h):
+            width = HALF // PER_COL
+            return offsets[:, h * width : (h + 1) * width]
+
+        def load_scale_rows(tile, source):
+            for q in range(QUADS):
+                nc.sync.dma_start(
+                    tile[32 * q : 32 * q + 4, :].bitcast(I32), source[0, 4 * q : 4 * q + 4, :].bitcast(I32)
+                )
+
+        def load_table(t):
+            tile = keep.tile([P, J], F32, name="tab%d" % t)
+            nc.sync.dma_start(tile[:], tab.rearrange("(p t) c -> p t c", t=PACK)[:, t, :])
+            return tile
+
+        x_bytes = keep.tile([P, T], U8, name="x_bytes", align_bytes=64)
+        nc.vector.memset(x_bytes[:].bitcast(I32), 0)
+        w_bytes_raw = []
+        for i in range(2):
+            tile = keep.tile([P, H], U8, name="w_bytes_raw%d" % i, align_bytes=64)
+            nc.gpsimd.memset(tile[:].bitcast(I32), 0)
+            w_bytes_raw.append(tile)
+        gain_rows = keep.tile([P, P], F32, name="gain_rows")
+        nc.gpsimd.memset(gain_rows[:], 0.0)
+        ident = keep.tile([P, P], F32, name="ident")
+        make_identity(nc, ident[:])
+
+        l5 = load_list(n5, "l5")
+        tabs = [load_table(0)]
+        l_offs = load_list(offs, "l_offs")
+        x_codes = keep.tile([P, T], U32, name="x_codes", align_bytes=64)
+        nc.sync.dma_start(x_codes[:].bitcast(I32), x_words[0].rearrange("p n t -> p (n t)").bitcast(I32))
+        load_scale_rows(x_bytes, x_scales)
+        tabs.append(load_table(1))
+        w_words_raw = [keep.tile([P, 2 * H], U8, name="w_words_raw%d" % i, align_bytes=64) for i in range(2)]
+        nc.sync.dma_start(w_words_raw[0][:].bitcast(I32), w1_words[0].bitcast(I32))
+        load_scale_rows(w_bytes_raw[0], w1_scales)
+        for i, gain in enumerate((ga, gb)):
+            nc.sync.dma_start(
+                gain_rows[PACK * i : PACK * (i + 1), :].rearrange("t (g e) -> t g e", e=8),
+                gain.rearrange("(g t e) o -> t g (e o)", t=PACK, e=8),
+            )
+        l_two = load_list(two, "l_two")
+        nc.sync.dma_start(w_words_raw[1][:].bitcast(I32), w2_words[0].bitcast(I32))
+        load_scale_rows(w_bytes_raw[1], w2_scales)
+        l1 = load_list(n1, "l1")
+        l3 = load_list(n3, "l3")
+        l4 = load_list(n4, "l4")
+        l2 = load_list(n2, "l2")
+        tabs.append(load_table(2))
+        tabs.append(load_table(3))
+        l7 = load_list(n7, "l7")
+        l6 = load_list(n6, "l6")
+
+        def fetch_factor(t, tile):
+            for h in range(2):
+                nc.vector.tensor_copy(tile[:, h * HALF : (h + 1) * HALF], tabs[t][:].indirect(half_of(l5, h)))
+
+        factors_early = keep.tile([P, 2, V], F32, name="factors_early")
+        factors = [factors_early[:, t, :] for t in range(2)]
+        for t in range(2):
+            fetch_factor(t, factors[t])
+
+        gain_bank = psum.tile([P, P], F32, name="bank")
+        nc.tensor.transpose(gain_bank[:], gain_rows[:], ident[:])
+        gains = keep.tile([P, 2 * PACK], F32, name="gains")
+        nc.scalar.copy(gains[:], gain_bank[:, 0 : 2 * PACK])
+        b_scale = keep.tile([P, PACK], F32, name="b_scale")
+        nc.scalar.activation(b_scale[:], gains[:, PACK:], ACT.Abs)
+        b_less_scale = keep.tile([P, PACK], F32, name="b_less_scale")
+        nc.scalar.activation(b_less_scale[:], gains[:, PACK:], ACT.Abs, scale=0.75)
+        half_sign = keep.tile([P, PACK], F32, name="half_sign")
+        nc.gpsimd.tensor_scalar(half_sign[:], gains[:, PACK:], 0.0, 0.5, ALU.is_lt, ALU.subtract)
+        a_half_scale = keep.tile([P, PACK], F32, name="a_half_scale")
+        nc.gpsimd.tensor_tensor(a_half_scale[:], half_sign[:], gains[:, :PACK], ALU.mult)
+        a_scale = keep.tile([P, PACK], F32, name="a_scale")
+        nc.gpsimd.tensor_scalar(a_scale[:], a_half_scale[:], 2.0, 0.0, ALU.mult, ALU.add)
+
+        def pick(offsets, name):
+            codes = keep.tile([P, COLS], U32, name=name + "_codes", align_bytes=64)
+            nc.vector.tensor_copy(codes[:], x_codes[:].indirect(offsets[:]))
+            scales = keep.tile([P, COLS], U8, name=name + "_scales", align_bytes=64)
+            nc.vector.tensor_copy(scales[:], x_bytes[:].indirect(offsets[:]))
+            return codes, scales
+
+        def deal(i):
+            words = keep.tile([P, 2 * H], U8, name="w_words%d" % i, align_bytes=64)
+            nc.vector.tensor_copy(
+                words[:].bitcast(I32).rearrange("p (t g j) -> p t g j", t=PACK, j=4),
+                w_words_raw[i][:].bitcast(I32).rearrange("p (g t j) -> p t g j", t=PACK, j=4),
+            )
+            scales = keep.tile([P, H], U8, name="w_bytes%d" % i, align_bytes=64)
+            nc.vector.tensor_copy(
+                scales[:].bitcast(I32).rearrange("p (t g j) -> p t g j", t=PACK, j=2),
+                w_bytes_raw[i][:].bitcast(I32).rearrange("p (g t j) -> p t g j", t=PACK, j=2),
+            )
+            return words, scales
+
+        def project(weights, picked, window_scale, plain_scale, name):
+            tiles = [keep.tile([P, 2 * COLS], F32, name="%s%d" % (name, t)) for t in range(PACK)]
+            for t in range(PACK):
+                bank = psum.tile([P, COLS], F32, name="bank")
+                nc.tensor.matmul_mx(
+                    out=bank[:],
+                    lhsT=weights[0][:, 2 * P * t : 2 * P * (t + 1)].bitcast(FP4X4),
+                    lhsT_scale=weights[1][:, P * t : P * (t + 1)],
+                    rhs=picked[0][:].bitcast(FP8X4),
+                    rhs_scale=picked[1][:],
+                    start=True,
+                    stop=True,
+                )
+                nc.scalar.activation(tiles[t ^ 1][:, COLS:], bank[:], ACT.Copy, scale=plain_scale[:, t : t + 1])
+                nc.scalar.activation(tiles[t][:, :COLS], bank[:], ACT.Copy, scale=window_scale[:, t : t + 1])
+            return tiles
+
+        picked_a = pick(l_offs, "xa")
+        weights_a = deal(0)
+        a_tiles = project(weights_a, picked_a, a_half_scale, a_scale, "a")
+        picked_b = pick(l_two, "xb")
+        weights_b = deal(1)
+        b_tiles = project(weights_b, picked_b, b_scale, b_less_scale, "b")
+
+        st_tiles = [keep.tile([P, 2 * COLS], F32, name="st%d" % t) for t in range(PACK)]
+        for t in range(PACK):
+            nc.vector.tensor_tensor(
+                st_tiles[t ^ 1][:, COLS:], a_tiles[t][:].indirect(l1[:]), a_tiles[t ^ 1][:, COLS:], ALU.add
+            )
+        for t in range(PACK):
+            nc.scalar.copy(st_tiles[t][:, :COLS], st_tiles[t ^ 1][:, COLS:])
+
+        by3 = keep.tile([P, PACK, COLS], F32, name="by3")
+        by4 = keep.tile([P, PACK, COLS], F32, name="by4")
+
+        def fetch_b(t):
+            for offsets, dest in ((l3, by3), (l4, by4)):
+                nc.vector.tensor_tensor(
+                    dest[:, t, :], b_tiles[t][:].indirect(offsets[:]), b_tiles[t ^ 1][:, COLS:], ALU.subtract
+                )
+
+        z_rows = keep.tile([P, PACK, COLS], F32, name="z_rows")
+        fetch_b(0)
+        fetch_b(1)
+        for t in range(PACK):
+            nc.vector.tensor_tensor(
+                z_rows[:, t, :], st_tiles[t][:].indirect(l2[:]), st_tiles[t ^ 1][:, COLS:], ALU.subtract
+            )
+        z_woven = keep.tile([P, PACK * COLS], BF16, name="z_woven", align_bytes=64)
+        nc.scalar.copy(
+            z_woven[:].rearrange("p (u m t) -> p m t u", u=PACK, t=PACK),
+            z_rows[:].rearrange("p t (m u) -> p m t u", u=PACK),
+        )
+        fetch_b(2)
+        fetch_b(3)
+
+        z2_woven = keep.tile([P, PACK * COLS], BF16, name="z2_woven", tag="z2_then_factors", align_bytes=64)
+        nc.vector.tensor_tensor(
+            z2_woven[:].rearrange("p (c i t) -> p c t i", i=4, t=PACK),
+            by3[:].rearrange("p t (c i) -> p c t i", i=4),
+            by4[:].rearrange("p t (c i) -> p c t i", i=4),
+            ALU.max,
+        )
+
+        def quantize(woven, codes, scales):
+            nc.vector.quantize_mx(out=codes.bitcast(FP8X4), scales=scales, in_=woven)
+
+        z_codes = keep.tile([P, COLS], U32, name="z_codes", align_bytes=64)
+        z_scales = keep.tile([P, COLS], U8, name="z_scales", align_bytes=64)
+        quantize(z_woven[:], z_codes[:], z_scales[:])
+        z2_codes = keep.tile([P, COLS], U32, name="z2_codes", align_bytes=64)
+        z2_scales = keep.tile([P, COLS], U8, name="z2_scales", align_bytes=64)
+        quantize(z2_woven[:], z2_codes[:], z2_scales[:])
+
+        s_tiles = []
+        for t in range(PACK):
+            bank = psum.tile([P, COLS], F32, name="bank")
+            nc.tensor.matmul_mx(
+                out=bank[:],
+                lhsT=z_codes[:, P * t : P * (t + 1)].bitcast(FP8X4),
+                lhsT_scale=z_scales[:, P * t : P * (t + 1)],
+                rhs=z2_codes[:].bitcast(FP8X4),
+                rhs_scale=z2_scales[:],
+                start=True,
+                stop=True,
+            )
+            tile = keep.tile([P, COLS], F32, name="s%d" % t)
+            nc.scalar.activation(tile[:], bank[:], ACT.Copy, scale=0.0625)
+            s_tiles.append(tile)
+
+        factors_late = keep.tile([P, 2, V], F32, name="factors_late", tag="z2_then_factors", align_bytes=64)
+        for t in range(2, PACK):
+            factors.append(factors_late[:, t - 2, :])
+            fetch_factor(t, factors[t])
+
+        out_rows = out_0.rearrange("(p t) c -> p t c", t=PACK)
+        out_codes = keep.tile([P, V], U32, name="out_codes", align_bytes=64)
+        out_scales = keep.tile([P, V], U8, name="out_scales", align_bytes=64)
+        words_out = out_1[0].rearrange("p n t -> p (n t)").bitcast(I32)
+        for h in range(2):
+            cols = slice(h * HALF, (h + 1) * HALF)
+            product = keep.tile([P, PACK, HALF], F32, name="product%d" % h)
+            result = keep.tile([P, PACK, HALF], F32, name="result%d" % h)
+            for t in range(PACK):
+                nc.vector.tensor_tensor(
+                    product[:, t, :], s_tiles[t][:].indirect(half_of(l7, h)), factors[t][:, cols], ALU.mult
+                )
+            for t in range(PACK):
+                nc.vector.tensor_tensor(
+                    result[:, t, :], tabs[t][:].indirect(half_of(l6, h)), product[:, t, :], ALU.add
+                )
+                nc.sync.dma_start(out_rows[:, t, cols], result[:, t, :])
+            woven = keep.tile([P, PACK * HALF], BF16, name="woven%d" % h, align_bytes=64)
+            woven_view = woven[:].rearrange("p (c i t) -> p c t i", i=4, t=PACK)
+            result_view = result[:].rearrange("p t (c i) -> p c t i", i=4)
+            if h == 0:
+                nc.scalar.copy(woven_view, result_view)
+            else:
+                nc.vector.tensor_copy(woven_view, result_view)
+            quantize(woven[:], out_codes[:, cols], out_scales[:, cols])
+            nc.sync.dma_start(words_out[:, cols], out_codes[:, cols].bitcast(I32))
+        for q in range(QUADS):
+            queue = nc.scalar if q % 2 == 0 else nc.sync
+            queue.dma_start(
+                out_2[0, 4 * q : 4 * q + 4, :].bitcast(I32), out_scales[32 * q : 32 * q + 4, :].bitcast(I32)
+            )

@@ -57,38 +57,37 @@ def tile_picked_kqhopoverkinda_none_po_kernel(
 
         x_bytes = keep.tile([P, T], U8, name="x_bytes", align_bytes=64)
         nc.vector.memset(x_bytes[:].bitcast(I32), 0)
+        gain_rows = keep.tile([P, P], F32, name="gain_rows")
+        nc.gpsimd.memset(gain_rows[:], 0.0)
+        for i, gain in enumerate((ga, gb)):
+            nc.gpsimd.dma_start(
+                gain_rows[PACK * i : PACK * (i + 1), :].rearrange("t (g e) -> t g e", e=8),
+                gain.rearrange("(g t e) o -> t g (e o)", t=PACK, e=8),
+            )
         w_bytes_raw = []
         for i in range(2):
             tile = keep.tile([P, H], U8, name="w_bytes_raw%d" % i, align_bytes=64)
-            nc.gpsimd.memset(tile[:].bitcast(I32), 0)
+            nc.vector.memset(tile[:].bitcast(I32), 0)
             w_bytes_raw.append(tile)
-        gain_rows = keep.tile([P, P], F32, name="gain_rows")
-        nc.gpsimd.memset(gain_rows[:], 0.0)
         ident = keep.tile([P, P], F32, name="ident")
         make_identity(nc, ident[:])
 
         l5 = load_list(n5, "l5")
-        tabs = [load_table(0)]
+        tabs = [load_table(0), load_table(1)]
         l_offs = load_list(offs, "l_offs")
         x_codes = keep.tile([P, T], U32, name="x_codes", align_bytes=64)
         nc.sync.dma_start(x_codes[:].bitcast(I32), x_words[0].rearrange("p n t -> p (n t)").bitcast(I32))
         load_scale_rows(x_bytes, x_scales)
-        tabs.append(load_table(1))
         w_words_raw = [keep.tile([P, 2 * H], U8, name="w_words_raw%d" % i, align_bytes=64) for i in range(2)]
         nc.sync.dma_start(w_words_raw[0][:].bitcast(I32), w1_words[0].bitcast(I32))
         load_scale_rows(w_bytes_raw[0], w1_scales)
-        for i, gain in enumerate((ga, gb)):
-            nc.sync.dma_start(
-                gain_rows[PACK * i : PACK * (i + 1), :].rearrange("t (g e) -> t g e", e=8),
-                gain.rearrange("(g t e) o -> t g (e o)", t=PACK, e=8),
-            )
         l_two = load_list(two, "l_two")
         nc.sync.dma_start(w_words_raw[1][:].bitcast(I32), w2_words[0].bitcast(I32))
         load_scale_rows(w_bytes_raw[1], w2_scales)
         l1 = load_list(n1, "l1")
+        l2 = load_list(n2, "l2")
         l3 = load_list(n3, "l3")
         l4 = load_list(n4, "l4")
-        l2 = load_list(n2, "l2")
         tabs.append(load_table(2))
         tabs.append(load_table(3))
         l7 = load_list(n7, "l7")
@@ -160,7 +159,6 @@ def tile_picked_kqhopoverkinda_none_po_kernel(
         a_tiles = project(weights_a, picked_a, a_half_scale, a_scale, "a")
         picked_b = pick(l_two, "xb")
         weights_b = deal(1)
-        b_tiles = project(weights_b, picked_b, b_scale, b_less_scale, "b")
 
         st_tiles = [keep.tile([P, 2 * COLS], F32, name="st%d" % t) for t in range(PACK)]
         for t in range(PACK):
@@ -170,6 +168,12 @@ def tile_picked_kqhopoverkinda_none_po_kernel(
         for t in range(PACK):
             nc.scalar.copy(st_tiles[t][:, :COLS], st_tiles[t ^ 1][:, COLS:])
 
+        z_rows = keep.tile([P, PACK, COLS], F32, name="z_rows")
+        for t in range(PACK):
+            nc.vector.tensor_tensor(
+                z_rows[:, t, :], st_tiles[t][:].indirect(l2[:]), st_tiles[t ^ 1][:, COLS:], ALU.subtract
+            )
+        b_tiles = project(weights_b, picked_b, b_scale, b_less_scale, "b")
         by3 = keep.tile([P, PACK, COLS], F32, name="by3")
         by4 = keep.tile([P, PACK, COLS], F32, name="by4")
 
@@ -179,20 +183,13 @@ def tile_picked_kqhopoverkinda_none_po_kernel(
                     dest[:, t, :], b_tiles[t][:].indirect(offsets[:]), b_tiles[t ^ 1][:, COLS:], ALU.subtract
                 )
 
-        z_rows = keep.tile([P, PACK, COLS], F32, name="z_rows")
-        fetch_b(0)
-        fetch_b(1)
-        for t in range(PACK):
-            nc.vector.tensor_tensor(
-                z_rows[:, t, :], st_tiles[t][:].indirect(l2[:]), st_tiles[t ^ 1][:, COLS:], ALU.subtract
-            )
         z_woven = keep.tile([P, PACK * COLS], BF16, name="z_woven", align_bytes=64)
         nc.scalar.copy(
             z_woven[:].rearrange("p (u m t) -> p m t u", u=PACK, t=PACK),
             z_rows[:].rearrange("p t (m u) -> p m t u", u=PACK),
         )
-        fetch_b(2)
-        fetch_b(3)
+        for t in range(PACK):
+            fetch_b(t)
 
         z2_woven = keep.tile([P, PACK * COLS], BF16, name="z2_woven", tag="z2_then_factors", align_bytes=64)
         nc.vector.tensor_tensor(

from contextlib import ExitStack

import concourse.mybir as mybir
from concourse.masks import make_identity

K, T, S, V, H, J = 512, 2048, 512, 512, 512, 512
FLOPS = 2 * K * H * S + 2 * K * H * V + 2 * H * S * V

F32 = mybir.dt.float32
BF16 = mybir.dt.bfloat16
I32 = mybir.dt.int32
U32 = mybir.dt.uint32
U16 = mybir.dt.uint16
U8 = mybir.dt.uint8
FP8X4 = mybir.dt.float8_e4m3fn_x4
FP4X4 = mybir.dt.float4_e2m1fn_x4
ALU = mybir.AluOpType
ACT = mybir.ActivationFunctionType

P = 128
PACK = 4
QUADS = 4
COLS = 512
HALF = COLS // 2
PER_COL = 16


def tile_picked_kqhopoverkinda_none_po_kernel(
    tc, x_words, x_scales, w1_words, w1_scales, w2_words, w2_scales, ga, gb, tab,
    offs, two, n1, n2, n3, n4, n5, n6, n7, out_0, out_1, out_2,
):
    nc = tc.nc
    with ExitStack() as ctx:
        lists = ctx.enter_context(tc.tile_pool(name="lists", bufs=1))
        keep = ctx.enter_context(tc.tile_pool(name="keep", bufs=1))
        psum = ctx.enter_context(tc.psum_pool(name="psum", bufs=8))

        def load_list(source, name):
            tile = lists.tile([P, COLS // PER_COL], U16, name=name)
            nc.sync.dma_start(tile[:], source)
            return tile

        def half_of(offsets, h):
            width = HALF // PER_COL
            return offsets[:, h * width : (h + 1) * width]

        def load_scale_rows(tile, source):
            for q in range(QUADS):
                nc.sync.dma_start(
                    tile[32 * q : 32 * q + 4, :].bitcast(I32), source[0, 4 * q : 4 * q + 4, :].bitcast(I32)
                )

        def load_table(t):
            tile = keep.tile([P, J], F32, name="tab%d" % t)
            nc.sync.dma_start(tile[:], tab.rearrange("(p t) c -> p t c", t=PACK)[:, t, :])
            return tile

        x_bytes = keep.tile([P, T], U8, name="x_bytes", align_bytes=64)
        nc.vector.memset(x_bytes[:].bitcast(I32), 0)
        gain_rows = keep.tile([P, P], F32, name="gain_rows")
        nc.gpsimd.memset(gain_rows[:], 0.0)
        for i, gain in enumerate((ga, gb)):
            nc.gpsimd.dma_start(
                gain_rows[PACK * i : PACK * (i + 1), :].rearrange("t (g e) -> t g e", e=8),
                gain.rearrange("(g t e) o -> t g (e o)", t=PACK, e=8),
            )
        w_bytes_raw = []
        for i in range(2):
            tile = keep.tile([P, H], U8, name="w_bytes_raw%d" % i, align_bytes=64)
            nc.vector.memset(tile[:].bitcast(I32), 0)
            w_bytes_raw.append(tile)
        ident = keep.tile([P, P], F32, name="ident")
        make_identity(nc, ident[:])

        l5 = load_list(n5, "l5")
        tabs = [load_table(0), load_table(1)]
        l_offs = load_list(offs, "l_offs")
        x_codes = keep.tile([P, T], U32, name="x_codes", align_bytes=64)
        nc.sync.dma_start(x_codes[:].bitcast(I32), x_words[0].rearrange("p n t -> p (n t)").bitcast(I32))
        load_scale_rows(x_bytes, x_scales)
        w_words_raw = [keep.tile([P, 2 * H], U8, name="w_words_raw%d" % i, align_bytes=64) for i in range(2)]
        nc.sync.dma_start(w_words_raw[0][:].bitcast(I32), w1_words[0].bitcast(I32))
        load_scale_rows(w_bytes_raw[0], w1_scales)
        l_two = load_list(two, "l_two")
        nc.sync.dma_start(w_words_raw[1][:].bitcast(I32), w2_words[0].bitcast(I32))
        load_scale_rows(w_bytes_raw[1], w2_scales)
        l1 = load_list(n1, "l1")
        l2 = load_list(n2, "l2")
        l3 = load_list(n3, "l3")
        l4 = load_list(n4, "l4")
        tabs.append(load_table(2))
        tabs.append(load_table(3))
        l7 = load_list(n7, "l7")
        l6 = load_list(n6, "l6")

        def fetch_factor(t, tile):
            for h in range(2):
                nc.vector.tensor_copy(tile[:, h * HALF : (h + 1) * HALF], tabs[t][:].indirect(half_of(l5, h)))

        factors_early = keep.tile([P, 2, V], F32, name="factors_early")
        factors = [factors_early[:, t, :] for t in range(2)]
        for t in range(2):
            fetch_factor(t, factors[t])

        gain_bank = psum.tile([P, P], F32, name="bank")
        nc.tensor.transpose(gain_bank[:], gain_rows[:], ident[:])
        gains = keep.tile([P, 2 * PACK], F32, name="gains")
        nc.scalar.copy(gains[:], gain_bank[:, 0 : 2 * PACK])
        b_scale = keep.tile([P, PACK], F32, name="b_scale")
        nc.scalar.activation(b_scale[:], gains[:, PACK:], ACT.Abs)
        b_less_scale = keep.tile([P, PACK], F32, name="b_less_scale")
        nc.scalar.activation(b_less_scale[:], gains[:, PACK:], ACT.Abs, scale=0.75)
        half_sign = keep.tile([P, PACK], F32, name="half_sign")
        nc.gpsimd.tensor_scalar(half_sign[:], gains[:, PACK:], 0.0, 0.5, ALU.is_lt, ALU.subtract)
        a_half_scale = keep.tile([P, PACK], F32, name="a_half_scale")
        nc.gpsimd.tensor_tensor(a_half_scale[:], half_sign[:], gains[:, :PACK], ALU.mult)
        a_scale = keep.tile([P, PACK], F32, name="a_scale")
        nc.gpsimd.tensor_scalar(a_scale[:], a_half_scale[:], 2.0, 0.0, ALU.mult, ALU.add)

        def pick(offsets, name):
            codes = keep.tile([P, COLS], U32, name=name + "_codes", align_bytes=64)
            nc.vector.tensor_copy(codes[:], x_codes[:].indirect(offsets[:]))
            scales = keep.tile([P, COLS], U8, name=name + "_scales", align_bytes=64)
            nc.vector.tensor_copy(scales[:], x_bytes[:].indirect(offsets[:]))
            return codes, scales

        def deal(i):
            words = keep.tile([P, 2 * H], U8, name="w_words%d" % i, align_bytes=64)
            nc.vector.tensor_copy(
                words[:].bitcast(I32).rearrange("p (t g j) -> p t g j", t=PACK, j=4),
                w_words_raw[i][:].bitcast(I32).rearrange("p (g t j) -> p t g j", t=PACK, j=4),
            )
            scales = keep.tile([P, H], U8, name="w_bytes%d" % i, align_bytes=64)
            nc.vector.tensor_copy(
                scales[:].bitcast(I32).rearrange("p (t g j) -> p t g j", t=PACK, j=2),
                w_bytes_raw[i][:].bitcast(I32).rearrange("p (g t j) -> p t g j", t=PACK, j=2),
            )
            return words, scales

        def project(weights, picked, window_scale, plain_scale, name):
            tiles = [keep.tile([P, 2 * COLS], F32, name="%s%d" % (name, t)) for t in range(PACK)]
            for t in range(PACK):
                bank = psum.tile([P, COLS], F32, name="bank")
                nc.tensor.matmul_mx(
                    out=bank[:],
                    lhsT=weights[0][:, 2 * P * t : 2 * P * (t + 1)].bitcast(FP4X4),
                    lhsT_scale=weights[1][:, P * t : P * (t + 1)],
                    rhs=picked[0][:].bitcast(FP8X4),
                    rhs_scale=picked[1][:],
                    start=True,
                    stop=True,
                )
                nc.scalar.activation(tiles[t ^ 1][:, COLS:], bank[:], ACT.Copy, scale=plain_scale[:, t : t + 1])
                nc.scalar.activation(tiles[t][:, :COLS], bank[:], ACT.Copy, scale=window_scale[:, t : t + 1])
            return tiles

        picked_a = pick(l_offs, "xa")
        weights_a = deal(0)
        a_tiles = project(weights_a, picked_a, a_half_scale, a_scale, "a")
        picked_b = pick(l_two, "xb")
        weights_b = deal(1)

        st_tiles = [keep.tile([P, 2 * COLS], F32, name="st%d" % t) for t in range(PACK)]
        for t in range(PACK):
            nc.vector.tensor_tensor(
                st_tiles[t ^ 1][:, COLS:], a_tiles[t][:].indirect(l1[:]), a_tiles[t ^ 1][:, COLS:], ALU.add
            )
        for t in range(PACK):
            nc.scalar.copy(st_tiles[t][:, :COLS], st_tiles[t ^ 1][:, COLS:])

        z_rows = keep.tile([P, PACK, COLS], F32, name="z_rows")
        for t in range(PACK):
            nc.vector.tensor_tensor(
                z_rows[:, t, :], st_tiles[t][:].indirect(l2[:]), st_tiles[t ^ 1][:, COLS:], ALU.subtract
            )
        b_tiles = project(weights_b, picked_b, b_scale, b_less_scale, "b")
        by3 = keep.tile([P, PACK, COLS], F32, name="by3")
        by4 = keep.tile([P, PACK, COLS], F32, name="by4")

        def fetch_b(t):
            for offsets, dest in ((l3, by3), (l4, by4)):
                nc.vector.tensor_tensor(
                    dest[:, t, :], b_tiles[t][:].indirect(offsets[:]), b_tiles[t ^ 1][:, COLS:], ALU.subtract
                )

        z_woven = keep.tile([P, PACK * COLS], BF16, name="z_woven", align_bytes=64)
        nc.scalar.copy(
            z_woven[:].rearrange("p (u m t) -> p m t u", u=PACK, t=PACK),
            z_rows[:].rearrange("p t (m u) -> p m t u", u=PACK),
        )
        for t in range(PACK):
            fetch_b(t)

        z2_woven = keep.tile([P, PACK * COLS], BF16, name="z2_woven", tag="z2_then_factors", align_bytes=64)
        nc.vector.tensor_tensor(
            z2_woven[:].rearrange("p (c i t) -> p c t i", i=4, t=PACK),
            by3[:].rearrange("p t (c i) -> p c t i", i=4),
            by4[:].rearrange("p t (c i) -> p c t i", i=4),
            ALU.max,
        )

        def quantize(woven, codes, scales):
            nc.vector.quantize_mx(out=codes.bitcast(FP8X4), scales=scales, in_=woven)

        z_codes = keep.tile([P, COLS], U32, name="z_codes", align_bytes=64)
        z_scales = keep.tile([P, COLS], U8, name="z_scales", align_bytes=64)
        quantize(z_woven[:], z_codes[:], z_scales[:])
        z2_codes = keep.tile([P, COLS], U32, name="z2_codes", align_bytes=64)
        z2_scales = keep.tile([P, COLS], U8, name="z2_scales", align_bytes=64)
        quantize(z2_woven[:], z2_codes[:], z2_scales[:])

        s_tiles = []
        for t in range(PACK):
            bank = psum.tile([P, COLS], F32, name="bank")
            nc.tensor.matmul_mx(
                out=bank[:],
                lhsT=z_codes[:, P * t : P * (t + 1)].bitcast(FP8X4),
                lhsT_scale=z_scales[:, P * t : P * (t + 1)],
                rhs=z2_codes[:].bitcast(FP8X4),
                rhs_scale=z2_scales[:],
                start=True,
                stop=True,
            )
            tile = keep.tile([P, COLS], F32, name="s%d" % t)
            nc.scalar.activation(tile[:], bank[:], ACT.Copy, scale=0.0625)
            s_tiles.append(tile)

        factors_late = keep.tile([P, 2, V], F32, name="factors_late", tag="z2_then_factors", align_bytes=64)
        for t in range(2, PACK):
            factors.append(factors_late[:, t - 2, :])
            fetch_factor(t, factors[t])

        out_rows = out_0.rearrange("(p t) c -> p t c", t=PACK)
        out_codes = keep.tile([P, V], U32, name="out_codes", align_bytes=64)
        out_scales = keep.tile([P, V], U8, name="out_scales", align_bytes=64)
        words_out = out_1[0].rearrange("p n t -> p (n t)").bitcast(I32)
        for h in range(2):
            cols = slice(h * HALF, (h + 1) * HALF)
            product = keep.tile([P, PACK, HALF], F32, name="product%d" % h)
            result = keep.tile([P, PACK, HALF], F32, name="result%d" % h)
            for t in range(PACK):
                nc.vector.tensor_tensor(
                    product[:, t, :], s_tiles[t][:].indirect(half_of(l7, h)), factors[t][:, cols], ALU.mult
                )
            for t in range(PACK):
                nc.vector.tensor_tensor(
                    result[:, t, :], tabs[t][:].indirect(half_of(l6, h)), product[:, t, :], ALU.add
                )
                nc.sync.dma_start(out_rows[:, t, cols], result[:, t, :])
            woven = keep.tile([P, PACK * HALF], BF16, name="woven%d" % h, align_bytes=64)
            woven_view = woven[:].rearrange("p (c i t) -> p c t i", i=4, t=PACK)
            result_view = result[:].rearrange("p t (c i) -> p c t i", i=4)
            if h == 0:
                nc.scalar.copy(woven_view, result_view)
            else:
                nc.vector.tensor_copy(woven_view, result_view)
            quantize(woven[:], out_codes[:, cols], out_scales[:, cols])
            nc.sync.dma_start(words_out[:, cols], out_codes[:, cols].bitcast(I32))
        for q in range(QUADS):
            queue = nc.scalar if q % 2 == 0 else nc.sync
            queue.dma_start(
                out_2[0, 4 * q : 4 * q + 4, :].bitcast(I32), out_scales[32 * q : 32 * q + 4, :].bitcast(I32)
            )
